import numpy as np
import ml_dtypes


def mxq(x, axis, fmt="e4m3"):
    dtype, down = {"e4m3": (ml_dtypes.float8_e4m3fn, 7), "e5m2": (ml_dtypes.float8_e5m2, 14)}[fmt]
    v = np.moveaxis(np.asarray(x, np.float32).astype(ml_dtypes.bfloat16).astype(np.float64), axis, -1)
    blocks = v.reshape(v.shape[:-1] + (-1, 32))
    amax = np.abs(blocks).max(-1, keepdims=True)
    byte = np.maximum(np.where(amax > 0, np.frexp(amax)[1] - 1 + 127, 0) - down, 1)
    scale = np.exp2(byte - 127.0)
    codes = (blocks / scale).astype(np.float32).astype(dtype).astype(np.float64)
    return np.moveaxis((codes * scale).reshape(v.shape), -1, axis)


WIDE = False


def mx_kscale(k):
    if not WIDE:
        return np.ones(k)
    levels = np.array([10, -10, 5, -5, 0])
    if k % 512:
        return np.exp2(np.random.permutation(np.resize(levels, k // 32))).repeat(32)
    a = np.empty((k // 512, 16))
    for p in range(k // 512):
        a[p, :8] = np.random.permutation(np.resize(levels, 8))
        for g in range(8):
            far = levels[np.abs(levels - a[p, g]) >= 10]
            a[p, g + 8] = far[np.random.randint(len(far))]
    return np.exp2(a.ravel()).repeat(32)


def f64(x):
    return np.asarray(x).astype(np.float64)


def striped(idx):
    return np.tile(idx.reshape(-1, 16).T, (8, 1)).astype(np.uint16)


def unstriped(offs):
    return offs[:16].T.reshape(-1).astype(np.int64)


def pack_weight(w):
    k, n = w.shape
    w = f64(np.asarray(w, np.float32).astype(ml_dtypes.bfloat16)).reshape(k // 32, 32, n)
    amax = np.abs(w).max(1)
    byte = np.clip(np.where(amax > 0, np.frexp(amax)[1] - 1 + 127 - 7, 1), 1, 254)
    scaled = (w * np.exp2(127.0 - byte)[:, None, :]).reshape(k, n).astype(np.float32)
    words = np.ascontiguousarray(scaled.reshape(k // 512, 128, 4, n).transpose(0, 1, 3, 2)).astype(ml_dtypes.float8_e4m3fn).view(np.uint8)
    return words, np.ascontiguousarray(byte.astype(np.uint8).reshape(k // 512, 16, n))


def unpack_weight(words, scales):
    g, p, n, _ = words.shape
    vals = np.ascontiguousarray(words).view(ml_dtypes.float8_e4m3fn).astype(np.float64) * np.repeat(np.exp2(scales.astype(np.float64) - 127.0), 8, axis=1)[..., None]
    return vals.transpose(0, 1, 3, 2).reshape(g * 512, n)


K, T, D, S, V, N = 1024, 1024, 8, 4096, 512, 128


def setup_inputs():
    n = np.random.standard_normal
    s = mx_kscale(K)[:, None]
    words, scales = pack_weight(n((K, N)) / np.sqrt(K) / s)
    return {
        "xT": (n((K, T)) * s).astype(np.float32),
        "w_words": words,
        "w_scales": scales,
        "offs": striped(np.concatenate([np.random.permutation(T)[:V] for _ in range(D)])),
    }


def reference(xT, w_words, w_scales, offs):
    w = unpack_weight(w_words, w_scales)
    idx = unstriped(offs)
    x = np.empty((K, V))
    for l in range(D):
        r = l // 4 * (4 * K // D) + l % 4 + 4 * np.arange(K // D)
        x[r] = f64(xT)[r][:, idx[l * V:(l + 1) * V]]
    xq = mxq(x, 0, "e4m3")
    return w.T @ xq

@@ -1,0 +1,125 @@
+from contextlib import ExitStack
+
+import concourse.mybir as mybir
+
+K, T, LEVELS, V, M = 1024, 1024, 8, 512, 128
+FLOPS = 2 * K * V * M
+
+F32 = mybir.dt.float32
+BF16 = mybir.dt.bfloat16
+I32 = mybir.dt.int32
+U32 = mybir.dt.uint32
+U16 = mybir.dt.uint16
+U8 = mybir.dt.uint8
+FP8X4 = mybir.dt.float8_e4m3fn_x4
+
+P = 128
+PACK = 4
+PASSES = 2
+GROUP = 16
+RUN = 4
+
+EARLY = slice(0, 128)
+DIRECT = slice(128, 384)
+LATE = slice(384, 512)
+PIECES = (EARLY, DIRECT, LATE)
+
+
+def tile_picked_grid_lin_none_sub_l_kernel(tc, xT, w_words, w_scales, offs, out):
+    nc = tc.nc
+    level_rows = xT.rearrange("(a f t) c -> a t f c", a=PASSES, t=PACK)
+
+    with ExitStack() as ctx:
+        keep = ctx.enter_context(tc.tile_pool(name="keep", bufs=1))
+        psum = ctx.enter_context(tc.psum_pool(name="psum", bufs=1))
+
+        offsets = keep.tile([P, LEVELS * V // GROUP], U16, name="offsets")
+        tables = [keep.tile([P, T], F32, name="table%d" % l) for l in range(LEVELS)]
+        picked = [keep.tile([P, PACK, V], F32, name="picked%d" % a) for a in range(PASSES)]
+        w_codes = keep.tile([P, PASSES, M], U32, name="w_codes", align_bytes=64)
+        w_plane = keep.tile([P, PASSES, M], U8, name="w_plane", align_bytes=64)
+        warm = keep.tile([P, 8], F32, name="warm")
+        rounded0 = keep.tile([P, V, PACK], BF16, name="rounded0", align_bytes=64)
+        codes0 = keep.tile([P, V], U32, name="codes0", align_bytes=64)
+        plane0 = keep.tile([P, V], U8, name="plane0", align_bytes=64)
+        rounded1, codes1, plane1, acc, result = {}, {}, {}, {}, {}
+        for piece in PIECES:
+            n = piece.stop - piece.start
+            s = piece.start
+            rounded1[s] = keep.tile([P, n, PACK], BF16, name="rounded1_%d" % s, align_bytes=64)
+            codes1[s] = keep.tile([P, n], U32, name="codes1_%d" % s, align_bytes=64)
+            plane1[s] = keep.tile([P, n], U8, name="plane1_%d" % s, align_bytes=64)
+            acc[s] = psum.tile([M, n], F32, name="acc%d" % s)
+            result[s] = keep.tile([M, n], F32, name="result%d" % s)
+
+        nc.sync.dma_start(tables[0][:], level_rows[0, 0])
+        nc.sync.dma_start(offsets[:], offs)
+        for l in range(1, LEVELS):
+            nc.sync.dma_start(tables[l][:], level_rows[l // PACK, l % PACK])
+        nc.sync.dma_start(
+            w_codes[:].bitcast(I32),
+            w_words.rearrange("a p m r -> p a (m r)").bitcast(I32),
+        )
+
+        nc.vector.memset(w_plane[:].rearrange("p a m -> p (a m)").bitcast(I32), 0)
+        nc.vector.memset(picked[1][:, PACK - 1, DIRECT], 0.0)
+        scale_rows = w_scales.rearrange("a (q r) m -> r q a m", r=4).bitcast(I32)
+        for r in range(4):
+            nc.scalar.dma_start(w_plane[r:P:32].bitcast(I32), scale_rows[r])
+        nc.scalar.copy(warm[:], picked[1][:, PACK - 1, DIRECT.start : DIRECT.start + 8])
+
+        def window(l, points):
+            first = (l * V + points.start) // GROUP
+            last = (l * V + points.stop) // GROUP
+            return tables[l][:].indirect(offsets[:, first:last])
+
+        def gather(l, points):
+            nc.vector.tensor_copy(picked[l // PACK][:, l % PACK, points], window(l, points))
+
+        def interleave(dst, a, points):
+            nc.scalar.copy(
+                dst.rearrange("p (c i) t -> p c t i", i=RUN),
+                picked[a][:, :, points].rearrange("p t (c i) -> p c t i", i=RUN),
+            )
+
+        def quantize(codes, plane, rounded):
+            nc.vector.quantize_mx(
+                out=codes[:].bitcast(FP8X4),
+                scales=plane[:],
+                in_=rounded[:].rearrange("p c t -> p (c t)"),
+            )
+
+        def multiply(piece, a, codes, plane):
+            nc.tensor.matmul_mx(
+                out=acc[piece.start][:],
+                lhsT=w_codes[:, a, :].bitcast(FP8X4),
+                lhsT_scale=w_plane[:, a, :],
+                rhs=codes.bitcast(FP8X4),
+                rhs_scale=plane,
+                start=(a == 0),
+                stop=(a == PASSES - 1),
+            )
+
+        every = slice(0, V)
+        for l in range(PACK):
+            gather(l, every)
+        interleave(rounded0[:], 0, every)
+        gather(4, every)
+        gather(5, every)
+        gather(6, DIRECT)
+        interleave(rounded1[DIRECT.start][:], 1, DIRECT)
+        gather(6, EARLY)
+        gather(6, LATE)
+        quantize(codes0, plane0, rounded0)
+        for piece in (EARLY, LATE):
+            gather(7, piece)
+            interleave(rounded1[piece.start][:], 1, piece)
+        nc.vector.tensor_copy(rounded1[DIRECT.start][:, :, PACK - 1], window(7, DIRECT))
+        for piece in PIECES:
+            multiply(piece, 0, codes0[:, piece], plane0[:, piece])
+        for piece in PIECES:
+            s = piece.start
+            quantize(codes1[s], plane1[s], rounded1[s])
+            multiply(piece, 1, codes1[s][:], plane1[s][:])
+            nc.scalar.copy(result[s][:], acc[s][:])
+            nc.sync.dma_start(out[:, piece], result[s][:])

@@ -19,10 +19,9 @@ PASSES = 2
 GROUP = 16
 RUN = 4
 
-EARLY = slice(0, 128)
-DIRECT = slice(128, 384)
-LATE = slice(384, 512)
-PIECES = (EARLY, DIRECT, LATE)
+PIECE = 128
+PIECES = [slice(s, s + PIECE) for s in range(0, V, PIECE)]
+ON_SCALAR = 4
 
 
 def tile_picked_grid_lin_none_sub_l_kernel(tc, xT, w_words, w_scales, offs, out):
@@ -38,55 +37,56 @@ def tile_picked_grid_lin_none_sub_l_kernel(tc, xT, w_words, w_scales, offs, out)
         picked = [keep.tile([P, PACK, V], F32, name="picked%d" % a) for a in range(PASSES)]
         w_codes = keep.tile([P, PASSES, M], U32, name="w_codes", align_bytes=64)
         w_plane = keep.tile([P, PASSES, M], U8, name="w_plane", align_bytes=64)
-        warm = keep.tile([P, 8], F32, name="warm")
+        warm = keep.tile([P, 16], F32, name="warm")
         rounded0 = keep.tile([P, V, PACK], BF16, name="rounded0", align_bytes=64)
         codes0 = keep.tile([P, V], U32, name="codes0", align_bytes=64)
         plane0 = keep.tile([P, V], U8, name="plane0", align_bytes=64)
-        rounded1, codes1, plane1, acc, result = {}, {}, {}, {}, {}
+        rounded1 = keep.tile([P, V, PACK], BF16, name="rounded1", align_bytes=64)
+        table_bf16 = keep.tile([P, T], BF16, name="table_bf16")
+        codes1, plane1, acc, result = {}, {}, {}, {}
         for piece in PIECES:
             n = piece.stop - piece.start
             s = piece.start
-            rounded1[s] = keep.tile([P, n, PACK], BF16, name="rounded1_%d" % s, align_bytes=64)
             codes1[s] = keep.tile([P, n], U32, name="codes1_%d" % s, align_bytes=64)
             plane1[s] = keep.tile([P, n], U8, name="plane1_%d" % s, align_bytes=64)
             acc[s] = psum.tile([M, n], F32, name="acc%d" % s)
             result[s] = keep.tile([M, n], F32, name="result%d" % s)
 
+        nc.vector.memset(w_plane[:].rearrange("p a m -> p (a m)").bitcast(I32), 0)
+        nc.vector.memset(warm[:, 0:8], 0.0)
+
         nc.sync.dma_start(tables[0][:], level_rows[0, 0])
         nc.sync.dma_start(offsets[:], offs)
-        for l in range(1, LEVELS):
+        for l in (1, 2, 3, 5, 4, 6, 7):
             nc.sync.dma_start(tables[l][:], level_rows[l // PACK, l % PACK])
+        scale_rows = w_scales.rearrange("a (q r) m -> r q a m", r=4).bitcast(I32)
+        for r in range(4):
+            nc.sync.dma_start(w_plane[r:P:32].bitcast(I32), scale_rows[r])
         nc.sync.dma_start(
             w_codes[:].bitcast(I32),
             w_words.rearrange("a p m r -> p a (m r)").bitcast(I32),
         )
+        nc.scalar.copy(warm[:, 8:16], warm[:, 0:8])
 
-        nc.vector.memset(w_plane[:].rearrange("p a m -> p (a m)").bitcast(I32), 0)
-        nc.vector.memset(picked[1][:, PACK - 1, DIRECT], 0.0)
-        scale_rows = w_scales.rearrange("a (q r) m -> r q a m", r=4).bitcast(I32)
-        for r in range(4):
-            nc.scalar.dma_start(w_plane[r:P:32].bitcast(I32), scale_rows[r])
-        nc.scalar.copy(warm[:], picked[1][:, PACK - 1, DIRECT.start : DIRECT.start + 8])
-
-        def window(l, points):
+        def window(table, l, points):
             first = (l * V + points.start) // GROUP
             last = (l * V + points.stop) // GROUP
-            return tables[l][:].indirect(offsets[:, first:last])
+            return table[:].indirect(offsets[:, first:last])
 
         def gather(l, points):
-            nc.vector.tensor_copy(picked[l // PACK][:, l % PACK, points], window(l, points))
+            nc.vector.tensor_copy(picked[l // PACK][:, l % PACK, points], window(tables[l], l, points))
 
-        def interleave(dst, a, points):
+        def interleave(dst, src):
             nc.scalar.copy(
                 dst.rearrange("p (c i) t -> p c t i", i=RUN),
-                picked[a][:, :, points].rearrange("p t (c i) -> p c t i", i=RUN),
+                src.rearrange("p t (c i) -> p c t i", i=RUN),
             )
 
         def quantize(codes, plane, rounded):
             nc.vector.quantize_mx(
                 out=codes[:].bitcast(FP8X4),
                 scales=plane[:],
-                in_=rounded[:].rearrange("p c t -> p (c t)"),
+                in_=rounded.rearrange("p c t -> p (c t)"),
             )
 
         def multiply(piece, a, codes, plane):
@@ -100,26 +100,43 @@ def tile_picked_grid_lin_none_sub_l_kernel(tc, xT, w_words, w_scales, offs, out)
                 stop=(a == PASSES - 1),
             )
 
+        def finish(piece, last=False):
+            s = piece.start
+            quantize(codes1[s], plane1[s], rounded1[:, piece, :])
+            multiply(piece, 1, codes1[s][:], plane1[s][:])
+            if last:
+                nc.vector.tensor_copy(result[s][:], acc[s][:])
+                nc.scalar.dma_start(out[:, piece], result[s][:])
+            else:
+                nc.scalar.copy(result[s][:], acc[s][:])
+                nc.sync.dma_start(out[:, piece], result[s][:])
+
         every = slice(0, V)
-        for l in range(PACK):
-            gather(l, every)
-        interleave(rounded0[:], 0, every)
-        gather(4, every)
+        shared = slice(0, V - PIECE)
+        own = PIECES[-1]
+        gather(0, every)
+        gather(1, every)
+        interleave(rounded0[:, :, 0:2], picked[0][:, 0:2, :])
+        gather(2, every)
+        for piece in PIECES:
+            gather(3, piece)
+            interleave(rounded0[:, piece, 2:4], picked[0][:, 2:4, piece])
         gather(5, every)
-        gather(6, DIRECT)
-        interleave(rounded1[DIRECT.start][:], 1, DIRECT)
-        gather(6, EARLY)
-        gather(6, LATE)
-        quantize(codes0, plane0, rounded0)
-        for piece in (EARLY, LATE):
-            gather(7, piece)
-            interleave(rounded1[piece.start][:], 1, piece)
-        nc.vector.tensor_copy(rounded1[DIRECT.start][:, :, PACK - 1], window(7, DIRECT))
+        nc.scalar.copy(table_bf16[:], tables[ON_SCALAR][:])
+        nc.scalar.activation(rounded1[:, shared, 0], window(table_bf16, ON_SCALAR, shared), mybir.ActivationFunctionType.Copy)
+        quantize(codes0, plane0, rounded0[:])
         for piece in PIECES:
             multiply(piece, 0, codes0[:, piece], plane0[:, piece])
-        for piece in PIECES:
-            s = piece.start
-            quantize(codes1[s], plane1[s], rounded1[s])
-            multiply(piece, 1, codes1[s][:], plane1[s][:])
-            nc.scalar.copy(result[s][:], acc[s][:])
-            nc.sync.dma_start(out[:, piece], result[s][:])
+        gather(ON_SCALAR, own)
+        gather(6, own)
+        gather(6, shared)
+        nc.vector.tensor_copy(
+            rounded1[:, own, 0:3].rearrange("p (c i) t -> p c t i", i=RUN),
+            picked[1][:, 0:3, own].rearrange("p t (c i) -> p c t i", i=RUN),
+        )
+        for piece in PIECES[:-1]:
+            gather(7, piece)
+            interleave(rounded1[:, piece, 1:], picked[1][:, 1:, piece])
+        nc.vector.tensor_copy(rounded1[:, own, 3], window(tables[7], 7, own))
+        for i in (0, 1, 3, 2):
+            finish(PIECES[i], last=(i == 2))

from contextlib import ExitStack

import concourse.mybir as mybir

K, T, LEVELS, V, M = 1024, 1024, 8, 512, 128
FLOPS = 2 * K * V * M

F32 = mybir.dt.float32
BF16 = mybir.dt.bfloat16
I32 = mybir.dt.int32
U32 = mybir.dt.uint32
U16 = mybir.dt.uint16
U8 = mybir.dt.uint8
FP8X4 = mybir.dt.float8_e4m3fn_x4

P = 128
PACK = 4
PASSES = 2
GROUP = 16
RUN = 4

PIECE = 128
PIECES = [slice(s, s + PIECE) for s in range(0, V, PIECE)]
ON_SCALAR = 4


def tile_picked_grid_lin_none_sub_l_kernel(tc, xT, w_words, w_scales, offs, out):
    nc = tc.nc
    level_rows = xT.rearrange("(a f t) c -> a t f c", a=PASSES, t=PACK)

    with ExitStack() as ctx:
        keep = ctx.enter_context(tc.tile_pool(name="keep", bufs=1))
        psum = ctx.enter_context(tc.psum_pool(name="psum", bufs=1))

        offsets = keep.tile([P, LEVELS * V // GROUP], U16, name="offsets")
        tables = [keep.tile([P, T], F32, name="table%d" % l) for l in range(LEVELS)]
        picked = [keep.tile([P, PACK, V], F32, name="picked%d" % a) for a in range(PASSES)]
        w_codes = keep.tile([P, PASSES, M], U32, name="w_codes", align_bytes=64)
        w_plane = keep.tile([P, PASSES, M], U8, name="w_plane", align_bytes=64)
        warm = keep.tile([P, 16], F32, name="warm")
        rounded0 = keep.tile([P, V, PACK], BF16, name="rounded0", align_bytes=64)
        codes0 = keep.tile([P, V], U32, name="codes0", align_bytes=64)
        plane0 = keep.tile([P, V], U8, name="plane0", align_bytes=64)
        rounded1 = keep.tile([P, V, PACK], BF16, name="rounded1", align_bytes=64)
        table_bf16 = keep.tile([P, T], BF16, name="table_bf16")
        codes1, plane1, acc, result = {}, {}, {}, {}
        for piece in PIECES:
            n = piece.stop - piece.start
            s = piece.start
            codes1[s] = keep.tile([P, n], U32, name="codes1_%d" % s, align_bytes=64)
            plane1[s] = keep.tile([P, n], U8, name="plane1_%d" % s, align_bytes=64)
            acc[s] = psum.tile([M, n], F32, name="acc%d" % s)
            result[s] = keep.tile([M, n], F32, name="result%d" % s)

        nc.vector.memset(w_plane[:].rearrange("p a m -> p (a m)").bitcast(I32), 0)
        nc.vector.memset(warm[:, 0:8], 0.0)

        nc.sync.dma_start(tables[0][:], level_rows[0, 0])
        nc.sync.dma_start(offsets[:], offs)
        for l in (1, 2, 3, 5, 4, 6, 7):
            nc.sync.dma_start(tables[l][:], level_rows[l // PACK, l % PACK])
        scale_rows = w_scales.rearrange("a (q r) m -> r q a m", r=4).bitcast(I32)
        for r in range(4):
            nc.sync.dma_start(w_plane[r:P:32].bitcast(I32), scale_rows[r])
        nc.sync.dma_start(
            w_codes[:].bitcast(I32),
            w_words.rearrange("a p m r -> p a (m r)").bitcast(I32),
        )
        nc.scalar.copy(warm[:, 8:16], warm[:, 0:8])

        def window(table, l, points):
            first = (l * V + points.start) // GROUP
            last = (l * V + points.stop) // GROUP
            return table[:].indirect(offsets[:, first:last])

        def gather(l, points):
            nc.vector.tensor_copy(picked[l // PACK][:, l % PACK, points], window(tables[l], l, points))

        def interleave(dst, src):
            nc.scalar.copy(
                dst.rearrange("p (c i) t -> p c t i", i=RUN),
                src.rearrange("p t (c i) -> p c t i", i=RUN),
            )

        def quantize(codes, plane, rounded):
            nc.vector.quantize_mx(
                out=codes[:].bitcast(FP8X4),
                scales=plane[:],
                in_=rounded.rearrange("p c t -> p (c t)"),
            )

        def multiply(piece, a, codes, plane):
            nc.tensor.matmul_mx(
                out=acc[piece.start][:],
                lhsT=w_codes[:, a, :].bitcast(FP8X4),
                lhsT_scale=w_plane[:, a, :],
                rhs=codes.bitcast(FP8X4),
                rhs_scale=plane,
                start=(a == 0),
                stop=(a == PASSES - 1),
            )

        def finish(piece, last=False):
            s = piece.start
            quantize(codes1[s], plane1[s], rounded1[:, piece, :])
            multiply(piece, 1, codes1[s][:], plane1[s][:])
            if last:
                nc.vector.tensor_copy(result[s][:], acc[s][:])
                nc.scalar.dma_start(out[:, piece], result[s][:])
            else:
                nc.scalar.copy(result[s][:], acc[s][:])
                nc.sync.dma_start(out[:, piece], result[s][:])

        every = slice(0, V)
        shared = slice(0, V - PIECE)
        own = PIECES[-1]
        gather(0, every)
        gather(1, every)
        interleave(rounded0[:, :, 0:2], picked[0][:, 0:2, :])
        gather(2, every)
        for piece in PIECES:
            gather(3, piece)
            interleave(rounded0[:, piece, 2:4], picked[0][:, 2:4, piece])
        gather(5, every)
        nc.scalar.copy(table_bf16[:], tables[ON_SCALAR][:])
        nc.scalar.activation(rounded1[:, shared, 0], window(table_bf16, ON_SCALAR, shared), mybir.ActivationFunctionType.Copy)
        quantize(codes0, plane0, rounded0[:])
        for piece in PIECES:
            multiply(piece, 0, codes0[:, piece], plane0[:, piece])
        gather(ON_SCALAR, own)
        gather(6, own)
        gather(6, shared)
        nc.vector.tensor_copy(
            rounded1[:, own, 0:3].rearrange("p (c i) t -> p c t i", i=RUN),
            picked[1][:, 0:3, own].rearrange("p t (c i) -> p c t i", i=RUN),
        )
        for piece in PIECES[:-1]:
            gather(7, piece)
            interleave(rounded1[:, piece, 1:], picked[1][:, 1:, piece])
        nc.vector.tensor_copy(rounded1[:, own, 3], window(tables[7], 7, own))
        for i in (0, 1, 3, 2):
            finish(PIECES[i], last=(i == 2))
